import numpy as np
import ml_dtypes


def mxq(x, axis, fmt="e4m3"):
    dtype, down = {"e4m3": (ml_dtypes.float8_e4m3fn, 7), "e5m2": (ml_dtypes.float8_e5m2, 14)}[fmt]
    v = np.moveaxis(np.asarray(x, np.float32).astype(ml_dtypes.bfloat16).astype(np.float64), axis, -1)
    blocks = v.reshape(v.shape[:-1] + (-1, 32))
    amax = np.abs(blocks).max(-1, keepdims=True)
    byte = np.maximum(np.where(amax > 0, np.frexp(amax)[1] - 1 + 127, 0) - down, 1)
    scale = np.exp2(byte - 127.0)
    codes = (blocks / scale).astype(np.float32).astype(dtype).astype(np.float64)
    return np.moveaxis((codes * scale).reshape(v.shape), -1, axis)


WIDE = False


def mx_kscale(k):
    if not WIDE:
        return np.ones(k)
    levels = np.array([24, -24, 12, -12, 0])
    if k % 512:
        return np.exp2(np.random.permutation(np.resize(levels, k // 32))).repeat(32)
    a = np.empty((k // 512, 16))
    for p in range(k // 512):
        a[p, :8] = np.random.permutation(np.resize(levels, 8))
        for g in range(8):
            far = levels[np.abs(levels - a[p, g]) >= 10]
            a[p, g + 8] = far[np.random.randint(len(far))]
    return np.exp2(a.ravel()).repeat(32)


def f64(x):
    return np.asarray(x).astype(np.float64)


def striped(idx):
    return np.tile(idx.reshape(-1, 16).T, (8, 1)).astype(np.uint16)


def unstriped(offs):
    return offs[:16].T.reshape(-1).astype(np.int64)


E2M1 = np.array([0.0, 0.5, 1.0, 1.5, 2.0, 3.0, 4.0, 6.0, -0.0, -0.5, -1.0, -1.5, -2.0, -3.0, -4.0, -6.0])


def pack_weight(w, fmt):
    k, n = w.shape
    w = f64(np.asarray(w, np.float32).astype(ml_dtypes.bfloat16)).reshape(k // 32, 32, n)
    amax = np.abs(w).max(1)
    if fmt == "e4m3":
        byte = np.frexp(amax)[1] - 1 + 127 - 7
    else:
        mant, ex = np.frexp(amax / 6.0)
        byte = np.where(mant > 0.5, ex, ex - 1) + 127
    byte = np.clip(np.where(amax > 0, byte, 1), 1, 254)
    scaled = (w * np.exp2(127.0 - byte)[:, None, :]).reshape(k, n).astype(np.float32)
    by_word = np.ascontiguousarray(scaled.reshape(k // 512, 128, 4, n).transpose(0, 1, 3, 2))
    if fmt == "e4m3":
        words = by_word.astype(ml_dtypes.float8_e4m3fn).view(np.uint8)
    else:
        c = by_word.astype(ml_dtypes.float4_e2m1fn).view(np.uint8) & 0xF
        words = (c[..., 0::2] | (c[..., 1::2] << 4)).reshape(k // 512, 128, 2 * n)
    return np.ascontiguousarray(words), np.ascontiguousarray(byte.astype(np.uint8).reshape(k // 512, 16, n))


def unpack_weight(words, scales, fmt):
    g, _, n = scales.shape
    words = np.ascontiguousarray(words).reshape(g, 128, n, -1)
    if fmt == "e4m3":
        vals = words.view(ml_dtypes.float8_e4m3fn).astype(np.float64)
    else:
        nib = np.empty((g, 128, n, 4), np.uint8)
        nib[..., 0::2] = words & 0xF
        nib[..., 1::2] = words >> 4
        vals = E2M1[nib]
    vals = vals * np.repeat(np.exp2(scales.astype(np.float64) - 127.0), 8, axis=1)[..., None]
    return vals.transpose(0, 1, 3, 2).reshape(g * 512, n)


def planes(y):
    n, m = y.shape
    v = y.astype(np.float32).astype(ml_dtypes.bfloat16).astype(np.float64).reshape(n // 32, 32, m)
    top = np.abs(v).max(1)
    byte = np.clip(np.where(top > 0, np.frexp(top)[1] - 1 + 127 - 7, 1), 1, 254)
    codes = (v * np.exp2(127.0 - byte)[:, None, :]).reshape(n, m).astype(np.float32).astype(ml_dtypes.float8_e4m3fn).view(np.uint8)
    words = codes.reshape(n // 512, 128, 4, m).transpose(0, 1, 3, 2)
    return np.ascontiguousarray(words), np.ascontiguousarray(byte.astype(np.uint8).reshape(n // 512, 16, m))


def sigm(f):
    return 1.0 / (1.0 + np.exp(-np.maximum(f, -700.0)))


K, L, N, T, J = 512, 512, 512, 2048, 1024


def setup_inputs():
    n = np.random.standard_normal
    s = mx_kscale(K)[:, None]
    s2 = mx_kscale(L)[:, None]
    p_tab = pack_weight(n((K, T)) * s, "e4m3")
    p_tab2 = pack_weight(n((L, T)) * s2, "e4m3")
    p_wv = pack_weight(n((K, N)) / np.sqrt(K) / s, "e4m3")
    p_wt = pack_weight(n((L, N)) / np.sqrt(L) / s2, "e2m1")
    return {
        "tab_words": p_tab[0],
        "tab_scales": p_tab[1],
        "tab2_words": p_tab2[0],
        "tab2_scales": p_tab2[1],
        "zv": (n((K, N)) / np.sqrt(K) / s).astype(np.float32),
        "zt": (n((L, N)) / np.sqrt(L) / s2).astype(np.float32),
        "b": (0.3 * n(N)).astype(np.float32),
        "wv_words": p_wv[0],
        "wv_scales": p_wv[1],
        "wt_words": p_wt[0],
        "wt_scales": p_wt[1],
        "wgo": np.tile(np.random.uniform(0.5, 2.0, J), (128, 1)).astype(np.float32),
        "offs": striped(np.random.permutation(T)[:J]),
        "offs2": striped(np.random.permutation(T)[:J]),
    }


def reference(tab_words, tab_scales, tab2_words, tab2_scales, zv, zt, b, wv_words, wv_scales, wt_words, wt_scales, wgo, offs, offs2):
    idx = unstriped(offs)
    idx2 = unstriped(offs2)
    tab_ = unpack_weight(tab_words, tab_scales, "e4m3")[:, idx]
    tab2_ = unpack_weight(tab2_words, tab2_scales, "e4m3")[:, idx2]
    zv_ = mxq(f64(zv), 0, "e4m3")
    zt_ = mxq(f64(zt), 0, "e4m3")
    z = zv_.T @ tab_ + zt_.T @ tab2_
    gate = sigm(z + f64(b)[:, None])
    wv_ = unpack_weight(wv_words, wv_scales, "e4m3")
    wt_ = unpack_weight(wt_words, wt_scales, "e2m1")
    hv = wv_.T @ tab_
    ht = wt_.T @ tab2_
    av = np.tanh(hv)
    at = np.tanh(ht)
    out = np.zeros((N, T))
    out[:, idx] = f64(wgo)[0] * (at + gate * (av - at))
    return (out,) + planes(out)

@@ -1,0 +1,246 @@
+from contextlib import ExitStack
+
+import concourse.mybir as mybir
+from concourse.masks import make_identity
+
+K, L, N, T, J = 512, 512, 512, 2048, 1024
+FLOPS = 2 * J * N * (2 * K + 2 * L)
+
+F32 = mybir.dt.float32
+BF16 = mybir.dt.bfloat16
+I32 = mybir.dt.int32
+U32 = mybir.dt.uint32
+U16 = mybir.dt.uint16
+U8 = mybir.dt.uint8
+FP8X4 = mybir.dt.float8_e4m3fn_x4
+FP4X4 = mybir.dt.float4_e2m1fn_x4
+ALU = mybir.AluOpType
+ACT = mybir.ActivationFunctionType
+
+P = 128
+PACK = 4
+CHUNK = 256
+BANK = 512
+OUT_COLS = 512
+
+
+def tile_list_gmu_tanh_scatP_kernel(
+    tc, tab_words, tab_scales, tab2_words, tab2_scales, zv, zt, b, wv_words, wv_scales,
+    wt_words, wt_scales, wgo, offs, offs2, out_0, out_1, out_2,
+):
+    nc = tc.nc
+    with ExitStack() as ctx:
+        keep = ctx.enter_context(tc.tile_pool(name="keep", bufs=1))
+        ring = ctx.enter_context(tc.tile_pool(name="ring", bufs=3))
+        shared = ctx.enter_context(tc.tile_pool(name="shared", bufs=1))
+        psum = ctx.enter_context(tc.psum_pool(name="psum", bufs=2))
+
+        list_v = keep.tile([P, J // 16], U16, name="list_v")
+        list_t = keep.tile([P, J // 16], U16, name="list_t")
+        slot = 4 * T
+        identity_draft = shared.tile([P, T * 4], F32, name="identity_draft", offset=0, align_bytes=64)
+        bias = shared.tile([P, PACK], F32, name="bias", offset=3 * slot + 3 * 1024, align_bytes=64)
+        w_rows = keep.tile([P, P], F32, name="w_rows")
+        table_words = [
+            keep.tile([P, T], I32, name="table_words0", align_bytes=64),
+            shared.tile([P, T], I32, name="table_words1", offset=2 * slot, align_bytes=64),
+        ]
+        table_scales = [keep.tile([P, T], U8, name="table_scales%d" % s, align_bytes=64) for s in range(2)]
+        picked_words = [keep.tile([P, J], U32, name="picked_words%d" % s, align_bytes=64) for s in range(2)]
+        picked_scales = [keep.tile([P, J], U8, name="picked_scales%d" % s, align_bytes=64) for s in range(2)]
+        wv_codes = shared.tile([P, N], I32, name="wv_codes", offset=3 * slot, align_bytes=64)
+        wt_codes = shared.tile([P, 2 * N], U8, name="wt_codes", offset=3 * slot + 2048, align_bytes=64)
+        w_scales = [keep.tile([P, N], U8, name="w_scales%d" % s, align_bytes=64) for s in range(2)]
+        z_raw = [
+            shared.tile([P, PACK, N], F32, name="z_raw0", offset=slot, align_bytes=64),
+            shared.tile([P, PACK, N], F32, name="z_raw1", offset=0, align_bytes=64),
+        ]
+        z_grouped = keep.tile([P, 2 * PACK * N], BF16, name="z_grouped", tag="late_page", align_bytes=64)
+        z_codes = [keep.tile([P, N], U32, name="z_codes%d" % s, align_bytes=64) for s in range(2)]
+        z_scales = [keep.tile([P, N], U8, name="z_scales%d" % s, align_bytes=64) for s in range(2)]
+        identity = keep.tile([P, P], F32, name="identity")
+        half_w = keep.tile([P, J // P], F32, name="half_w")
+        half_bias = keep.tile([P, PACK], F32, name="half_bias")
+        pages = [keep.tile([P, T], F32, name="page%d" % t, align_bytes=64) for t in range(PACK - 1)]
+        scaled = [[None] * (J // P) for s in range(2)]
+        for i in range(J // P):
+            for s in range(2):
+                if i // 2 == 1 and s == 1:
+                    scaled[s][i] = shared.tile([P, PACK, P], F32, name="scaled%d_%d" % (s, i), offset=(i % 2) * 4 * N, align_bytes=64)
+                else:
+                    scaled[s][i] = keep.tile([P, PACK, P], F32, name="scaled%d_%d" % (s, i))
+        blocks = [slice(c, c + OUT_COLS) for c in range(0, T, OUT_COLS)]
+        pairs = [keep.tile([P, OUT_COLS * PACK], BF16, name="pairs%d" % k, align_bytes=64) for k in range(len(blocks))]
+        y_grouped = [keep.tile([P, OUT_COLS * PACK], BF16, name="y_grouped%d" % k, align_bytes=64) for k in range(len(blocks))]
+        y_codes = [keep.tile([P, OUT_COLS], U32, name="y_codes%d" % k, align_bytes=64) for k in range(len(blocks))]
+        y_scales = keep.tile([P, T], U8, name="y_scales", align_bytes=64)
+        lists = [list_v, list_t]
+
+        def load_scale_rows(queue, plane, rows):
+            for q in range(4):
+                queue.dma_start(out=plane[32 * q : 32 * q + 4, :].bitcast(I32), in_=rows[0, 4 * q : 4 * q + 4, :].bitcast(I32))
+
+        def as_words(dram):
+            return dram[0].rearrange("p n t -> p (n t)").bitcast(I32)
+
+        for plane in table_scales:
+            nc.vector.memset(plane[:].bitcast(I32), 0)
+        nc.gpsimd.memset(w_rows[:], 0.0)
+        make_identity(nc, identity_draft[:, 0:P])
+        nc.gpsimd.tensor_copy(identity[:], identity_draft[:, 0:P])
+        for plane in w_scales:
+            nc.gpsimd.memset(plane[:].bitcast(I32), 0)
+
+        nc.sync.dma_start(list_v[:], offs)
+        nc.sync.dma_start(out=table_words[0][:], in_=as_words(tab_words))
+        nc.sync.dma_start(list_t[:], offs2)
+        nc.sync.dma_start(out=w_rows[0 : J // P, :], in_=wgo[0].rearrange("(i c) -> i c", c=P))
+        load_scale_rows(nc.sync, table_scales[0], tab_scales)
+        nc.sync.dma_start(out=wv_codes[:], in_=as_words(wv_words))
+        nc.sync.dma_start(out=z_raw[0][:], in_=zv.rearrange("(p j) n -> p j n", j=PACK))
+        nc.sync.dma_start(out=table_words[1][:], in_=as_words(tab2_words))
+        nc.sync.dma_start(out=wt_codes[:].bitcast(I32), in_=wt_words[0].bitcast(I32))
+        load_scale_rows(nc.sync, table_scales[1], tab2_scales)
+        nc.sync.dma_start(out=z_raw[1][:], in_=zt.rearrange("(p j) n -> p j n", j=PACK))
+        nc.sync.dma_start(out=bias[:], in_=b.rearrange("(p t) -> p t", t=PACK))
+        load_scale_rows(nc.gpsimd, w_scales[0], wv_scales)
+        load_scale_rows(nc.gpsimd, w_scales[1], wt_scales)
+        nc.gpsimd.tensor_scalar(half_bias[:], bias[:], 0.5, 0.0, ALU.mult, ALU.add)
+
+        for page in pages:
+            nc.vector.memset(page[:], 0.0)
+
+        w_bank = psum.tile([P, BANK], F32, name="w_bank", tag="diff")
+        nc.tensor.transpose(w_bank[:, 0:P], w_rows[:], identity[:])
+        nc.vector.tensor_scalar(half_w[:], w_bank[:, 0 : J // P], 0.5, None, ALU.mult)
+
+        def gather(first, count):
+            for s in range(2):
+                offsets = lists[s][:, first // 16 : (first + count) // 16]
+                nc.vector.tensor_copy(picked_scales[s][:, first : first + count], table_scales[s][:].indirect(offsets))
+                nc.vector.tensor_copy(picked_words[s][:, first : first + count], table_words[s][:].bitcast(U32).indirect(offsets))
+
+        def quantise_gate_weight(s, copy):
+            grouped = z_grouped[:, s * PACK * N : (s + 1) * PACK * N]
+            copy(
+                grouped.rearrange("p (t m j) -> p m j t", t=PACK, j=PACK),
+                z_raw[s][:].rearrange("p j (m t) -> p m j t", t=PACK),
+            )
+            nc.vector.quantize_mx(out=z_codes[s][:].bitcast(FP8X4), scales=z_scales[s][:], in_=grouped)
+
+        branch_weights = (wv_codes[:].bitcast(FP8X4), wt_codes[:].bitcast(FP4X4))
+
+        def branch(s, i):
+            items = slice(i * P, (i + 1) * P)
+            h = psum.tile([P, BANK], F32, name="h")
+            nc.tensor.matmul_mx(
+                out=h[:], lhsT=picked_words[s][:, items].bitcast(FP8X4), lhsT_scale=picked_scales[s][:, items],
+                rhs=branch_weights[s], rhs_scale=w_scales[s][:], start=True, stop=True,
+            )
+            a = scaled[s][i]
+            nc.scalar.activation(a[:], h[:].rearrange("p (m t) -> p t m", t=PACK), ACT.Tanh, scale=1.0 - 2.0 * s)
+            nc.scalar.activation(a[:], a[:], ACT.Copy, scale=half_w[:, i : i + 1])
+
+        def branches(i):
+            branch(0, i)
+            branch(1, i)
+
+        def combine(runs):
+            z = psum.tile([P, BANK], F32, name="z")
+            text = psum.tile([P, BANK], F32, name="text")
+            diff = psum.tile([P, BANK], F32, name="diff", tag="diff")
+            gate_tanh = ring.tile([P, BANK], F32, name="gate_tanh")
+            base = ring.tile([P, BANK], F32, name="base")
+            gated = ring.tile([P, BANK], F32, name="gated")
+            col = 0
+            for t, first, count in runs:
+                rows = slice(t * P, (t + 1) * P)
+                items = slice(first, first + count)
+                for s in range(2):
+                    nc.tensor.matmul_mx(
+                        out=z[:, col : col + count], lhsT=z_codes[s][:, rows].bitcast(FP8X4), lhsT_scale=z_scales[s][:, rows],
+                        rhs=picked_words[s][:, items].bitcast(FP8X4), rhs_scale=picked_scales[s][:, items],
+                        start=(s == 0), stop=(s == 1),
+                    )
+                col += count
+            col = 0
+            for t, first, count in runs:
+                for i in range(first // P, (first + count) // P):
+                    nc.tensor.transpose(text[:, col : col + P], scaled[1][i][:, t, :], identity[:])
+                    col += P
+            col = 0
+            for t, first, count in runs:
+                for i in range(first // P, (first + count) // P):
+                    for s in range(2):
+                        nc.tensor.matmul(diff[:, col : col + P], scaled[s][i][:, t, :], identity[:], start=(s == 0), stop=(s == 1), is_transpose=True)
+                    col += P
+            col = 0
+            for t, first, count in runs:
+                nc.scalar.activation(gate_tanh[:, col : col + count], z[:, col : col + count], ACT.Tanh, bias=half_bias[:, t : t + 1], scale=0.5)
+                col += count
+            nc.scalar.activation(base[:], text[:], ACT.Copy, scale=-2.0)
+            nc.vector.scalar_tensor_tensor(gated[:], gate_tanh[:], 1.0, diff[:], ALU.add, ALU.mult)
+            col = 0
+            for t, first, count in runs:
+                offsets = list_v[:, first // 16 : (first + count) // 16]
+                nc.vector.tensor_tensor(pages[t][:].indirect(offsets), gated[:, col : col + count], base[:, col : col + count], ALU.add)
+                col += count
+
+        out_pages = out_0.rearrange("(p t) c -> t p c", t=PACK)
+
+        def store_page(t):
+            nc.sync.dma_start(out=out_pages[t], in_=pages[t][:])
+
+        def round_page(t):
+            for k, cols in enumerate(blocks):
+                slots = pairs[k][:].rearrange("p (u c e) -> p u c e", u=2, e=2)
+                nc.scalar.copy(slots[:, t // 2, :, t % 2], pages[t][:, cols])
+
+        gather(0, CHUNK)
+        quantise_gate_weight(0, nc.scalar.copy)
+        quantise_gate_weight(1, nc.vector.tensor_copy)
+        gather(CHUNK, CHUNK)
+        gather(2 * CHUNK, 2 * CHUNK)
+        last_page = keep.tile([P, T], F32, name="last_page", tag="late_page", align_bytes=64)
+        pages.append(last_page)
+        nc.gpsimd.memset(last_page[:], 0.0)
+
+        branches(0)
+        branches(1)
+        branch(0, 2)
+        branch(0, 3)
+        branch(1, 2)
+        combine([(0, 0, CHUNK), (1, 0, CHUNK)])
+        branch(1, 3)
+        combine([(2, 0, CHUNK), (3, 0, CHUNK)])
+        combine([(0, CHUNK, CHUNK), (1, CHUNK, CHUNK)])
+        branches(4)
+        branches(5)
+        combine([(2, CHUNK, CHUNK), (3, CHUNK, CHUNK)])
+        branches(6)
+        combine([(0, 2 * CHUNK, CHUNK), (1, 2 * CHUNK, CHUNK)])
+        branches(7)
+        combine([(0, 3 * CHUNK, CHUNK), (1, 3 * CHUNK, CHUNK)])
+        store_page(0)
+        store_page(1)
+        combine([(2, 2 * CHUNK, 2 * CHUNK)])
+        store_page(2)
+        combine([(3, 2 * CHUNK, 2 * CHUNK)])
+        store_page(3)
+        for t in range(PACK):
+            round_page(t)
+
+        code_rows = as_words(out_1)
+        for k, cols in enumerate(blocks):
+            if k < len(blocks) - 1:
+                copy, word = nc.vector.tensor_copy, I32
+            else:
+                copy, word = nc.scalar.copy, U32
+            copy(
+                y_grouped[k][:].bitcast(word).rearrange("p (c u) -> p c u", u=2),
+                pairs[k][:].bitcast(word).rearrange("p (u c) -> p c u", u=2),
+            )
+            nc.vector.quantize_mx(out=y_codes[k][:].bitcast(FP8X4), scales=y_scales[:, cols], in_=y_grouped[k][:])
+            nc.sync.dma_start(out=code_rows[:, cols], in_=y_codes[k][:].bitcast(I32))
+        for q in range(4):
+            nc.sync.dma_start(out=out_2[0, 4 * q : 4 * q + 4, :].bitcast(I32), in_=y_scales[32 * q : 32 * q + 4, :].bitcast(I32))

@@ -38,7 +38,7 @@ def tile_list_gmu_tanh_scatP_kernel(
         list_v = keep.tile([P, J // 16], U16, name="list_v")
         list_t = keep.tile([P, J // 16], U16, name="list_t")
         slot = 4 * T
-        identity_draft = shared.tile([P, T * 4], F32, name="identity_draft", offset=0, align_bytes=64)
+        identity_draft = shared.tile([P, T * 6], F32, name="identity_draft", offset=0, align_bytes=64)
         bias = shared.tile([P, PACK], F32, name="bias", offset=3 * slot + 3 * 1024, align_bytes=64)
         w_rows = keep.tile([P, P], F32, name="w_rows")
         table_words = [
@@ -46,8 +46,18 @@ def tile_list_gmu_tanh_scatP_kernel(
             shared.tile([P, T], I32, name="table_words1", offset=2 * slot, align_bytes=64),
         ]
         table_scales = [keep.tile([P, T], U8, name="table_scales%d" % s, align_bytes=64) for s in range(2)]
-        picked_words = [keep.tile([P, J], U32, name="picked_words%d" % s, align_bytes=64) for s in range(2)]
-        picked_scales = [keep.tile([P, J], U8, name="picked_scales%d" % s, align_bytes=64) for s in range(2)]
+        half = J // 2
+        word_halves = [[keep.tile([P, half], U32, name="picked_words%d_%d" % (s, u), align_bytes=64) for u in range(2 - s)] for s in range(2)]
+        scale_halves = [[keep.tile([P, half], U8, name="picked_scales%d_%d" % (s, u), align_bytes=64) for u in range(2 - s)] for s in range(2)]
+        word_halves[1].append(shared.tile([P, half], U32, name="picked_words1_1", offset=4096, align_bytes=64))
+        scale_halves[1].append(shared.tile([P, half], U8, name="picked_scales1_1", offset=4096 + 2048, align_bytes=64))
+
+        def picked_words(s, first, count):
+            return word_halves[s][first // half][:, first % half : first % half + count]
+
+        def picked_scales(s, first, count):
+            return scale_halves[s][first // half][:, first % half : first % half + count]
+
         wv_codes = shared.tile([P, N], I32, name="wv_codes", offset=3 * slot, align_bytes=64)
         wt_codes = shared.tile([P, 2 * N], U8, name="wt_codes", offset=3 * slot + 2048, align_bytes=64)
         w_scales = [keep.tile([P, N], U8, name="w_scales%d" % s, align_bytes=64) for s in range(2)]
@@ -55,18 +65,19 @@ def tile_list_gmu_tanh_scatP_kernel(
             shared.tile([P, PACK, N], F32, name="z_raw0", offset=slot, align_bytes=64),
             shared.tile([P, PACK, N], F32, name="z_raw1", offset=0, align_bytes=64),
         ]
-        z_grouped = keep.tile([P, 2 * PACK * N], BF16, name="z_grouped", tag="late_page", align_bytes=64)
+        z_grouped = shared.tile([P, 2 * PACK * N], BF16, name="z_grouped", offset=6 * slot, align_bytes=64)
         z_codes = [keep.tile([P, N], U32, name="z_codes%d" % s, align_bytes=64) for s in range(2)]
         z_scales = [keep.tile([P, N], U8, name="z_scales%d" % s, align_bytes=64) for s in range(2)]
         identity = keep.tile([P, P], F32, name="identity")
-        half_w = keep.tile([P, J // P], F32, name="half_w")
         half_bias = keep.tile([P, PACK], F32, name="half_bias")
-        pages = [keep.tile([P, T], F32, name="page%d" % t, align_bytes=64) for t in range(PACK - 1)]
+        half_w = keep.tile([P, J // P], F32, name="half_w")
+        pages = [keep.tile([P, T], F32, name="page%d" % t, align_bytes=64) for t in range(2)]
+        pages += [shared.tile([P, T], F32, name="page%d" % t, offset=(2 + t) * slot, align_bytes=64) for t in range(2, PACK)]
         scaled = [[None] * (J // P) for s in range(2)]
         for i in range(J // P):
             for s in range(2):
                 if i // 2 == 1 and s == 1:
-                    scaled[s][i] = shared.tile([P, PACK, P], F32, name="scaled%d_%d" % (s, i), offset=(i % 2) * 4 * N, align_bytes=64)
+                    scaled[s][i] = shared.tile([P, PACK, P], F32, name="scaled%d_%d" % (s, i), offset=6 * slot + 4 * N * (2 + i % 2), align_bytes=64)
                 else:
                     scaled[s][i] = keep.tile([P, PACK, P], F32, name="scaled%d_%d" % (s, i))
         blocks = [slice(c, c + OUT_COLS) for c in range(0, T, OUT_COLS)]
@@ -83,32 +94,33 @@ def tile_list_gmu_tanh_scatP_kernel(
         def as_words(dram):
             return dram[0].rearrange("p n t -> p (n t)").bitcast(I32)
 
-        for plane in table_scales:
+        for plane in (table_scales[0], w_scales[0], table_scales[1]):
             nc.vector.memset(plane[:].bitcast(I32), 0)
         nc.gpsimd.memset(w_rows[:], 0.0)
+        nc.gpsimd.memset(w_scales[1][:].bitcast(I32), 0)
         make_identity(nc, identity_draft[:, 0:P])
         nc.gpsimd.tensor_copy(identity[:], identity_draft[:, 0:P])
-        for plane in w_scales:
-            nc.gpsimd.memset(plane[:].bitcast(I32), 0)
 
         nc.sync.dma_start(list_v[:], offs)
         nc.sync.dma_start(out=table_words[0][:], in_=as_words(tab_words))
         nc.sync.dma_start(list_t[:], offs2)
         nc.sync.dma_start(out=w_rows[0 : J // P, :], in_=wgo[0].rearrange("(i c) -> i c", c=P))
         load_scale_rows(nc.sync, table_scales[0], tab_scales)
-        nc.sync.dma_start(out=wv_codes[:], in_=as_words(wv_words))
         nc.sync.dma_start(out=z_raw[0][:], in_=zv.rearrange("(p j) n -> p j n", j=PACK))
+        nc.sync.dma_start(out=wv_codes[:], in_=as_words(wv_words))
+        load_scale_rows(nc.sync, w_scales[0], wv_scales)
         nc.sync.dma_start(out=table_words[1][:], in_=as_words(tab2_words))
         nc.sync.dma_start(out=wt_codes[:].bitcast(I32), in_=wt_words[0].bitcast(I32))
         load_scale_rows(nc.sync, table_scales[1], tab2_scales)
         nc.sync.dma_start(out=z_raw[1][:], in_=zt.rearrange("(p j) n -> p j n", j=PACK))
         nc.sync.dma_start(out=bias[:], in_=b.rearrange("(p t) -> p t", t=PACK))
-        load_scale_rows(nc.gpsimd, w_scales[0], wv_scales)
         load_scale_rows(nc.gpsimd, w_scales[1], wt_scales)
-        nc.gpsimd.tensor_scalar(half_bias[:], bias[:], 0.5, 0.0, ALU.mult, ALU.add)
 
-        for page in pages:
-            nc.vector.memset(page[:], 0.0)
+        for page in pages[:2]:
+            nc.vector.memset(page[:].bitcast(I32), 0)
+        for page in pages[2:]:
+            nc.gpsimd.memset(page[:].bitcast(I32), 0)
+        nc.gpsimd.tensor_scalar(half_bias[:], bias[:], 0.5, 0.0, ALU.mult, ALU.add)
 
         w_bank = psum.tile([P, BANK], F32, name="w_bank", tag="diff")
         nc.tensor.transpose(w_bank[:, 0:P], w_rows[:], identity[:])
@@ -117,28 +129,27 @@ def tile_list_gmu_tanh_scatP_kernel(
         def gather(first, count):
             for s in range(2):
                 offsets = lists[s][:, first // 16 : (first + count) // 16]
-                nc.vector.tensor_copy(picked_scales[s][:, first : first + count], table_scales[s][:].indirect(offsets))
-                nc.vector.tensor_copy(picked_words[s][:, first : first + count], table_words[s][:].bitcast(U32).indirect(offsets))
+                nc.vector.tensor_copy(picked_scales(s, first, count), table_scales[s][:].indirect(offsets))
+                nc.vector.tensor_copy(picked_words(s, first, count), table_words[s][:].bitcast(U32).indirect(offsets))
 
         def quantise_gate_weight(s, copy):
             grouped = z_grouped[:, s * PACK * N : (s + 1) * PACK * N]
             copy(
-                grouped.rearrange("p (t m j) -> p m j t", t=PACK, j=PACK),
-                z_raw[s][:].rearrange("p j (m t) -> p m j t", t=PACK),
+                grouped.rearrange("p (t m j) -> p m t j", t=PACK, j=PACK),
+                z_raw[s][:].rearrange("p j (m t) -> p m t j", t=PACK),
             )
             nc.vector.quantize_mx(out=z_codes[s][:].bitcast(FP8X4), scales=z_scales[s][:], in_=grouped)
 
         branch_weights = (wv_codes[:].bitcast(FP8X4), wt_codes[:].bitcast(FP4X4))
 
         def branch(s, i):
-            items = slice(i * P, (i + 1) * P)
             h = psum.tile([P, BANK], F32, name="h")
             nc.tensor.matmul_mx(
-                out=h[:], lhsT=picked_words[s][:, items].bitcast(FP8X4), lhsT_scale=picked_scales[s][:, items],
+                out=h[:], lhsT=picked_words(s, i * P, P).bitcast(FP8X4), lhsT_scale=picked_scales(s, i * P, P),
                 rhs=branch_weights[s], rhs_scale=w_scales[s][:], start=True, stop=True,
             )
             a = scaled[s][i]
-            nc.scalar.activation(a[:], h[:].rearrange("p (m t) -> p t m", t=PACK), ACT.Tanh, scale=1.0 - 2.0 * s)
+            nc.scalar.activation(a[:].rearrange("p t m -> p m t"), h[:].rearrange("p (m t) -> p m t", t=PACK), ACT.Tanh, scale=1.0 - 2.0 * s)
             nc.scalar.activation(a[:], a[:], ACT.Copy, scale=half_w[:, i : i + 1])
 
         def branches(i):
@@ -149,17 +160,16 @@ def tile_list_gmu_tanh_scatP_kernel(
             z = psum.tile([P, BANK], F32, name="z")
             text = psum.tile([P, BANK], F32, name="text")
             diff = psum.tile([P, BANK], F32, name="diff", tag="diff")
-            gate_tanh = ring.tile([P, BANK], F32, name="gate_tanh")
+            gate = ring.tile([P, BANK], F32, name="gate")
             base = ring.tile([P, BANK], F32, name="base")
             gated = ring.tile([P, BANK], F32, name="gated")
             col = 0
             for t, first, count in runs:
                 rows = slice(t * P, (t + 1) * P)
-                items = slice(first, first + count)
                 for s in range(2):
                     nc.tensor.matmul_mx(
                         out=z[:, col : col + count], lhsT=z_codes[s][:, rows].bitcast(FP8X4), lhsT_scale=z_scales[s][:, rows],
-                        rhs=picked_words[s][:, items].bitcast(FP8X4), rhs_scale=picked_scales[s][:, items],
+                        rhs=picked_words(s, first, count).bitcast(FP8X4), rhs_scale=picked_scales(s, first, count),
                         start=(s == 0), stop=(s == 1),
                     )
                 col += count
@@ -176,10 +186,11 @@ def tile_list_gmu_tanh_scatP_kernel(
                     col += P
             col = 0
             for t, first, count in runs:
-                nc.scalar.activation(gate_tanh[:, col : col + count], z[:, col : col + count], ACT.Tanh, bias=half_bias[:, t : t + 1], scale=0.5)
+                nc.scalar.activation(gate[:, col : col + count], z[:, col : col + count], ACT.Tanh, bias=half_bias[:, t : t + 1], scale=0.5)
                 col += count
             nc.scalar.activation(base[:], text[:], ACT.Copy, scale=-2.0)
-            nc.vector.scalar_tensor_tensor(gated[:], gate_tanh[:], 1.0, diff[:], ALU.add, ALU.mult)
+            for cols in (slice(0, CHUNK), slice(CHUNK, BANK)):
+                nc.vector.scalar_tensor_tensor(gated[:, cols], gate[:, cols], 1.0, diff[:, cols], ALU.add, ALU.mult)
             col = 0
             for t, first, count in runs:
                 offsets = list_v[:, first // 16 : (first + count) // 16]
@@ -201,24 +212,21 @@ def tile_list_gmu_tanh_scatP_kernel(
         quantise_gate_weight(1, nc.vector.tensor_copy)
         gather(CHUNK, CHUNK)
         gather(2 * CHUNK, 2 * CHUNK)
-        last_page = keep.tile([P, T], F32, name="last_page", tag="late_page", align_bytes=64)
-        pages.append(last_page)
-        nc.gpsimd.memset(last_page[:], 0.0)
 
         branches(0)
         branches(1)
         branch(0, 2)
         branch(0, 3)
-        branch(1, 2)
         combine([(0, 0, CHUNK), (1, 0, CHUNK)])
-        branch(1, 3)
         combine([(2, 0, CHUNK), (3, 0, CHUNK)])
+        branch(1, 2)
+        branch(1, 3)
         combine([(0, CHUNK, CHUNK), (1, CHUNK, CHUNK)])
         branches(4)
-        branches(5)
         combine([(2, CHUNK, CHUNK), (3, CHUNK, CHUNK)])
-        branches(6)
+        branches(5)
         combine([(0, 2 * CHUNK, CHUNK), (1, 2 * CHUNK, CHUNK)])
+        branches(6)
         branches(7)
         combine([(0, 3 * CHUNK, CHUNK), (1, 3 * CHUNK, CHUNK)])
         store_page(0)

@@ -49,8 +49,8 @@ def tile_list_gmu_tanh_scatP_kernel(
         half = J // 2
         word_halves = [[keep.tile([P, half], U32, name="picked_words%d_%d" % (s, u), align_bytes=64) for u in range(2 - s)] for s in range(2)]
         scale_halves = [[keep.tile([P, half], U8, name="picked_scales%d_%d" % (s, u), align_bytes=64) for u in range(2 - s)] for s in range(2)]
-        word_halves[1].append(shared.tile([P, half], U32, name="picked_words1_1", offset=4096, align_bytes=64))
-        scale_halves[1].append(shared.tile([P, half], U8, name="picked_scales1_1", offset=4096 + 2048, align_bytes=64))
+        word_halves[1].append(shared.tile([P, half], U32, name="picked_words1_1", offset=6 * slot, align_bytes=64))
+        scale_halves[1].append(shared.tile([P, half], U8, name="picked_scales1_1", offset=6 * slot + 2048, align_bytes=64))
 
         def picked_words(s, first, count):
             return word_halves[s][first // half][:, first % half : first % half + count]
@@ -66,8 +66,8 @@ def tile_list_gmu_tanh_scatP_kernel(
             shared.tile([P, PACK, N], F32, name="z_raw1", offset=0, align_bytes=64),
         ]
         z_grouped = shared.tile([P, 2 * PACK * N], BF16, name="z_grouped", offset=6 * slot, align_bytes=64)
-        z_codes = [keep.tile([P, N], U32, name="z_codes%d" % s, align_bytes=64) for s in range(2)]
-        z_scales = [keep.tile([P, N], U8, name="z_scales%d" % s, align_bytes=64) for s in range(2)]
+        z_codes = keep.tile([P, 2 * N], U32, name="z_codes", align_bytes=64)
+        z_scales = keep.tile([P, 2 * N], U8, name="z_scales", align_bytes=64)
         identity = keep.tile([P, P], F32, name="identity")
         half_bias = keep.tile([P, PACK], F32, name="half_bias")
         half_w = keep.tile([P, J // P], F32, name="half_w")
@@ -138,7 +138,6 @@ def tile_list_gmu_tanh_scatP_kernel(
                 grouped.rearrange("p (t m j) -> p m t j", t=PACK, j=PACK),
                 z_raw[s][:].rearrange("p j (m t) -> p m t j", t=PACK),
             )
-            nc.vector.quantize_mx(out=z_codes[s][:].bitcast(FP8X4), scales=z_scales[s][:], in_=grouped)
 
         branch_weights = (wv_codes[:].bitcast(FP8X4), wt_codes[:].bitcast(FP4X4))
 
@@ -165,10 +164,10 @@ def tile_list_gmu_tanh_scatP_kernel(
             gated = ring.tile([P, BANK], F32, name="gated")
             col = 0
             for t, first, count in runs:
-                rows = slice(t * P, (t + 1) * P)
                 for s in range(2):
+                    rows = slice(s * N + t * P, s * N + (t + 1) * P)
                     nc.tensor.matmul_mx(
-                        out=z[:, col : col + count], lhsT=z_codes[s][:, rows].bitcast(FP8X4), lhsT_scale=z_scales[s][:, rows],
+                        out=z[:, col : col + count], lhsT=z_codes[:, rows].bitcast(FP8X4), lhsT_scale=z_scales[:, rows],
                         rhs=picked_words(s, first, count).bitcast(FP8X4), rhs_scale=picked_scales(s, first, count),
                         start=(s == 0), stop=(s == 1),
                     )
@@ -205,11 +204,13 @@ def tile_list_gmu_tanh_scatP_kernel(
         def round_page(t):
             for k, cols in enumerate(blocks):
                 slots = pairs[k][:].rearrange("p (u c e) -> p u c e", u=2, e=2)
-                nc.scalar.copy(slots[:, t // 2, :, t % 2], pages[t][:, cols])
+                copy = nc.vector.tensor_copy if (t >= 2 and k == len(blocks) - 1) else nc.scalar.copy
+                copy(slots[:, t // 2, :, t % 2], pages[t][:, cols])
 
         gather(0, CHUNK)
         quantise_gate_weight(0, nc.scalar.copy)
         quantise_gate_weight(1, nc.vector.tensor_copy)
+        nc.vector.quantize_mx(out=z_codes[:].bitcast(FP8X4), scales=z_scales[:], in_=z_grouped[:])
         gather(CHUNK, CHUNK)
         gather(2 * CHUNK, 2 * CHUNK)
 
@@ -239,16 +240,24 @@ def tile_list_gmu_tanh_scatP_kernel(
             round_page(t)
 
         code_rows = as_words(out_1)
-        for k, cols in enumerate(blocks):
-            if k < len(blocks) - 1:
-                copy, word = nc.vector.tensor_copy, I32
-            else:
-                copy, word = nc.scalar.copy, U32
+
+        def interleave(k, copy, word):
             copy(
                 y_grouped[k][:].bitcast(word).rearrange("p (c u) -> p c u", u=2),
                 pairs[k][:].bitcast(word).rearrange("p (u c) -> p c u", u=2),
             )
-            nc.vector.quantize_mx(out=y_codes[k][:].bitcast(FP8X4), scales=y_scales[:, cols], in_=y_grouped[k][:])
-            nc.sync.dma_start(out=code_rows[:, cols], in_=y_codes[k][:].bitcast(I32))
+
+        def quantise_block(k):
+            nc.vector.quantize_mx(out=y_codes[k][:].bitcast(FP8X4), scales=y_scales[:, blocks[k]], in_=y_grouped[k][:])
+            nc.sync.dma_start(out=code_rows[:, blocks[k]], in_=y_codes[k][:].bitcast(I32))
+
+        interleave(3, nc.vector.tensor_copy, I32)
+        interleave(0, nc.vector.tensor_copy, I32)
+        quantise_block(3)
+        interleave(1, nc.vector.tensor_copy, I32)
+        quantise_block(0)
+        interleave(2, nc.scalar.copy, U32)
+        quantise_block(1)
+        quantise_block(2)
         for q in range(4):
-            nc.sync.dma_start(out=out_2[0, 4 * q : 4 * q + 4, :].bitcast(I32), in_=y_scales[32 * q : 32 * q + 4, :].bitcast(I32))
+            nc.scalar.dma_start(out=out_2[0, 4 * q : 4 * q + 4, :].bitcast(I32), in_=y_scales[32 * q : 32 * q + 4, :].bitcast(I32))

@@ -47,9 +47,8 @@ def tile_list_gmu_tanh_scatP_kernel(
         ]
         table_scales = [keep.tile([P, T], U8, name="table_scales%d" % s, align_bytes=64) for s in range(2)]
         half = J // 2
-        word_halves = [[keep.tile([P, half], U32, name="picked_words%d_%d" % (s, u), align_bytes=64) for u in range(2 - s)] for s in range(2)]
+        word_halves = [[keep.tile([P, half], U32, name="picked_words%d_%d" % (s, u), align_bytes=64) for u in range(2)] for s in range(2)]
         scale_halves = [[keep.tile([P, half], U8, name="picked_scales%d_%d" % (s, u), align_bytes=64) for u in range(2 - s)] for s in range(2)]
-        word_halves[1].append(shared.tile([P, half], U32, name="picked_words1_1", offset=6 * slot, align_bytes=64))
         scale_halves[1].append(shared.tile([P, half], U8, name="picked_scales1_1", offset=6 * slot + 2048, align_bytes=64))
 
         def picked_words(s, first, count):
@@ -61,10 +60,8 @@ def tile_list_gmu_tanh_scatP_kernel(
         wv_codes = shared.tile([P, N], I32, name="wv_codes", offset=3 * slot, align_bytes=64)
         wt_codes = shared.tile([P, 2 * N], U8, name="wt_codes", offset=3 * slot + 2048, align_bytes=64)
         w_scales = [keep.tile([P, N], U8, name="w_scales%d" % s, align_bytes=64) for s in range(2)]
-        z_raw = [
-            shared.tile([P, PACK, N], F32, name="z_raw0", offset=slot, align_bytes=64),
-            shared.tile([P, PACK, N], F32, name="z_raw1", offset=0, align_bytes=64),
-        ]
+        zv_raw = shared.tile([P, PACK, N], F32, name="zv_raw", offset=slot, align_bytes=64)
+        zt_raw = [shared.tile([P, PACK, N // 2], F32, name="zt_raw%d" % u, offset=u * slot // 2, align_bytes=64) for u in range(2)]
         z_grouped = shared.tile([P, 2 * PACK * N], BF16, name="z_grouped", offset=6 * slot, align_bytes=64)
         z_codes = keep.tile([P, 2 * N], U32, name="z_codes", align_bytes=64)
         z_scales = keep.tile([P, 2 * N], U8, name="z_scales", align_bytes=64)
@@ -76,8 +73,8 @@ def tile_list_gmu_tanh_scatP_kernel(
         scaled = [[None] * (J // P) for s in range(2)]
         for i in range(J // P):
             for s in range(2):
-                if i // 2 == 1 and s == 1:
-                    scaled[s][i] = shared.tile([P, PACK, P], F32, name="scaled%d_%d" % (s, i), offset=6 * slot + 4 * N * (2 + i % 2), align_bytes=64)
+                if i == 2:
+                    scaled[s][i] = shared.tile([P, PACK, P], F32, name="scaled%d_%d" % (s, i), offset=6 * slot + 4 * N * (2 + s), align_bytes=64)
                 else:
                     scaled[s][i] = keep.tile([P, PACK, P], F32, name="scaled%d_%d" % (s, i))
         blocks = [slice(c, c + OUT_COLS) for c in range(0, T, OUT_COLS)]
@@ -106,13 +103,14 @@ def tile_list_gmu_tanh_scatP_kernel(
         nc.sync.dma_start(list_t[:], offs2)
         nc.sync.dma_start(out=w_rows[0 : J // P, :], in_=wgo[0].rearrange("(i c) -> i c", c=P))
         load_scale_rows(nc.sync, table_scales[0], tab_scales)
-        nc.sync.dma_start(out=z_raw[0][:], in_=zv.rearrange("(p j) n -> p j n", j=PACK))
+        nc.sync.dma_start(out=zv_raw[:], in_=zv.rearrange("(p j) n -> p j n", j=PACK))
         nc.sync.dma_start(out=wv_codes[:], in_=as_words(wv_words))
         load_scale_rows(nc.sync, w_scales[0], wv_scales)
         nc.sync.dma_start(out=table_words[1][:], in_=as_words(tab2_words))
         nc.sync.dma_start(out=wt_codes[:].bitcast(I32), in_=wt_words[0].bitcast(I32))
         load_scale_rows(nc.sync, table_scales[1], tab2_scales)
-        nc.sync.dma_start(out=z_raw[1][:], in_=zt.rearrange("(p j) n -> p j n", j=PACK))
+        for u in range(2):
+            nc.sync.dma_start(out=zt_raw[u][:], in_=zt[:, u * N // 2 : (u + 1) * N // 2].rearrange("(p j) n -> p j n", j=PACK))
         nc.sync.dma_start(out=bias[:], in_=b.rearrange("(p t) -> p t", t=PACK))
         load_scale_rows(nc.gpsimd, w_scales[1], wt_scales)
 
@@ -132,12 +130,13 @@ def tile_list_gmu_tanh_scatP_kernel(
                 nc.vector.tensor_copy(picked_scales(s, first, count), table_scales[s][:].indirect(offsets))
                 nc.vector.tensor_copy(picked_words(s, first, count), table_words[s][:].bitcast(U32).indirect(offsets))
 
-        def quantise_gate_weight(s, copy):
+        def quantise_gate_weight(s, raw_halves, copies):
             grouped = z_grouped[:, s * PACK * N : (s + 1) * PACK * N]
-            copy(
-                grouped.rearrange("p (t m j) -> p m t j", t=PACK, j=PACK),
-                z_raw[s][:].rearrange("p j (m t) -> p m t j", t=PACK),
-            )
+            dealt = grouped.rearrange("p (t m j) -> p m t j", t=PACK, j=PACK)
+            for u in range(2):
+                copies[u](dealt[:, u * P // 2 : (u + 1) * P // 2], raw_halves[u].rearrange("p j (m t) -> p m t j", t=PACK))
+            cols = slice(s * N, (s + 1) * N)
+            nc.vector.quantize_mx(out=z_codes[:, cols].bitcast(FP8X4), scales=z_scales[:, cols], in_=grouped)
 
         branch_weights = (wv_codes[:].bitcast(FP8X4), wt_codes[:].bitcast(FP4X4))
 
@@ -208,20 +207,17 @@ def tile_list_gmu_tanh_scatP_kernel(
                 copy(slots[:, t // 2, :, t % 2], pages[t][:, cols])
 
         gather(0, CHUNK)
-        quantise_gate_weight(0, nc.scalar.copy)
-        quantise_gate_weight(1, nc.vector.tensor_copy)
-        nc.vector.quantize_mx(out=z_codes[:].bitcast(FP8X4), scales=z_scales[:], in_=z_grouped[:])
+        quantise_gate_weight(0, [zv_raw[:, :, 0 : N // 2], zv_raw[:, :, N // 2 : N]], [nc.scalar.copy, nc.vector.tensor_copy])
+        quantise_gate_weight(1, [zt_raw[0][:], zt_raw[1][:]], [nc.vector.tensor_copy, nc.vector.tensor_copy])
         gather(CHUNK, CHUNK)
         gather(2 * CHUNK, 2 * CHUNK)
 
         branches(0)
         branches(1)
-        branch(0, 2)
-        branch(0, 3)
         combine([(0, 0, CHUNK), (1, 0, CHUNK)])
         combine([(2, 0, CHUNK), (3, 0, CHUNK)])
-        branch(1, 2)
-        branch(1, 3)
+        branches(2)
+        branches(3)
         combine([(0, CHUNK, CHUNK), (1, CHUNK, CHUNK)])
         branches(4)
         combine([(2, CHUNK, CHUNK), (3, CHUNK, CHUNK)])

from contextlib import ExitStack

import concourse.mybir as mybir
from concourse.masks import make_identity

K, L, N, T, J = 512, 512, 512, 2048, 1024
FLOPS = 2 * J * N * (2 * K + 2 * L)

F32 = mybir.dt.float32
BF16 = mybir.dt.bfloat16
I32 = mybir.dt.int32
U32 = mybir.dt.uint32
U16 = mybir.dt.uint16
U8 = mybir.dt.uint8
FP8X4 = mybir.dt.float8_e4m3fn_x4
FP4X4 = mybir.dt.float4_e2m1fn_x4
ALU = mybir.AluOpType
ACT = mybir.ActivationFunctionType

P = 128
PACK = 4
CHUNK = 256
BANK = 512
OUT_COLS = 512


def tile_list_gmu_tanh_scatP_kernel(
    tc, tab_words, tab_scales, tab2_words, tab2_scales, zv, zt, b, wv_words, wv_scales,
    wt_words, wt_scales, wgo, offs, offs2, out_0, out_1, out_2,
):
    nc = tc.nc
    with ExitStack() as ctx:
        keep = ctx.enter_context(tc.tile_pool(name="keep", bufs=1))
        ring = ctx.enter_context(tc.tile_pool(name="ring", bufs=3))
        shared = ctx.enter_context(tc.tile_pool(name="shared", bufs=1))
        psum = ctx.enter_context(tc.psum_pool(name="psum", bufs=2))

        list_v = keep.tile([P, J // 16], U16, name="list_v")
        list_t = keep.tile([P, J // 16], U16, name="list_t")
        slot = 4 * T
        identity_draft = shared.tile([P, T * 6], F32, name="identity_draft", offset=0, align_bytes=64)
        bias = shared.tile([P, PACK], F32, name="bias", offset=3 * slot + 3 * 1024, align_bytes=64)
        w_rows = keep.tile([P, P], F32, name="w_rows")
        table_words = [
            keep.tile([P, T], I32, name="table_words0", align_bytes=64),
            shared.tile([P, T], I32, name="table_words1", offset=2 * slot, align_bytes=64),
        ]
        table_scales = [keep.tile([P, T], U8, name="table_scales%d" % s, align_bytes=64) for s in range(2)]
        half = J // 2
        word_halves = [[keep.tile([P, half], U32, name="picked_words%d_%d" % (s, u), align_bytes=64) for u in range(2)] for s in range(2)]
        scale_halves = [[keep.tile([P, half], U8, name="picked_scales%d_%d" % (s, u), align_bytes=64) for u in range(2 - s)] for s in range(2)]
        scale_halves[1].append(shared.tile([P, half], U8, name="picked_scales1_1", offset=6 * slot + 2048, align_bytes=64))

        def picked_words(s, first, count):
            return word_halves[s][first // half][:, first % half : first % half + count]

        def picked_scales(s, first, count):
            return scale_halves[s][first // half][:, first % half : first % half + count]

        wv_codes = shared.tile([P, N], I32, name="wv_codes", offset=3 * slot, align_bytes=64)
        wt_codes = shared.tile([P, 2 * N], U8, name="wt_codes", offset=3 * slot + 2048, align_bytes=64)
        w_scales = [keep.tile([P, N], U8, name="w_scales%d" % s, align_bytes=64) for s in range(2)]
        zv_raw = shared.tile([P, PACK, N], F32, name="zv_raw", offset=slot, align_bytes=64)
        zt_raw = [shared.tile([P, PACK, N // 2], F32, name="zt_raw%d" % u, offset=u * slot // 2, align_bytes=64) for u in range(2)]
        z_grouped = shared.tile([P, 2 * PACK * N], BF16, name="z_grouped", offset=6 * slot, align_bytes=64)
        z_codes = keep.tile([P, 2 * N], U32, name="z_codes", align_bytes=64)
        z_scales = keep.tile([P, 2 * N], U8, name="z_scales", align_bytes=64)
        identity = keep.tile([P, P], F32, name="identity")
        half_bias = keep.tile([P, PACK], F32, name="half_bias")
        half_w = keep.tile([P, J // P], F32, name="half_w")
        pages = [keep.tile([P, T], F32, name="page%d" % t, align_bytes=64) for t in range(2)]
        pages += [shared.tile([P, T], F32, name="page%d" % t, offset=(2 + t) * slot, align_bytes=64) for t in range(2, PACK)]
        scaled = [[None] * (J // P) for s in range(2)]
        for i in range(J // P):
            for s in range(2):
                if i == 2:
                    scaled[s][i] = shared.tile([P, PACK, P], F32, name="scaled%d_%d" % (s, i), offset=6 * slot + 4 * N * (2 + s), align_bytes=64)
                else:
                    scaled[s][i] = keep.tile([P, PACK, P], F32, name="scaled%d_%d" % (s, i))
        blocks = [slice(c, c + OUT_COLS) for c in range(0, T, OUT_COLS)]
        pairs = [keep.tile([P, OUT_COLS * PACK], BF16, name="pairs%d" % k, align_bytes=64) for k in range(len(blocks))]
        y_grouped = [keep.tile([P, OUT_COLS * PACK], BF16, name="y_grouped%d" % k, align_bytes=64) for k in range(len(blocks))]
        y_codes = [keep.tile([P, OUT_COLS], U32, name="y_codes%d" % k, align_bytes=64) for k in range(len(blocks))]
        y_scales = keep.tile([P, T], U8, name="y_scales", align_bytes=64)
        lists = [list_v, list_t]

        def load_scale_rows(queue, plane, rows):
            for q in range(4):
                queue.dma_start(out=plane[32 * q : 32 * q + 4, :].bitcast(I32), in_=rows[0, 4 * q : 4 * q + 4, :].bitcast(I32))

        def as_words(dram):
            return dram[0].rearrange("p n t -> p (n t)").bitcast(I32)

        for plane in (table_scales[0], w_scales[0], table_scales[1]):
            nc.vector.memset(plane[:].bitcast(I32), 0)
        nc.gpsimd.memset(w_rows[:], 0.0)
        nc.gpsimd.memset(w_scales[1][:].bitcast(I32), 0)
        make_identity(nc, identity_draft[:, 0:P])
        nc.gpsimd.tensor_copy(identity[:], identity_draft[:, 0:P])

        nc.sync.dma_start(list_v[:], offs)
        nc.sync.dma_start(out=table_words[0][:], in_=as_words(tab_words))
        nc.sync.dma_start(list_t[:], offs2)
        nc.sync.dma_start(out=w_rows[0 : J // P, :], in_=wgo[0].rearrange("(i c) -> i c", c=P))
        load_scale_rows(nc.sync, table_scales[0], tab_scales)
        nc.sync.dma_start(out=zv_raw[:], in_=zv.rearrange("(p j) n -> p j n", j=PACK))
        nc.sync.dma_start(out=wv_codes[:], in_=as_words(wv_words))
        load_scale_rows(nc.sync, w_scales[0], wv_scales)
        nc.sync.dma_start(out=table_words[1][:], in_=as_words(tab2_words))
        nc.sync.dma_start(out=wt_codes[:].bitcast(I32), in_=wt_words[0].bitcast(I32))
        load_scale_rows(nc.sync, table_scales[1], tab2_scales)
        for u in range(2):
            nc.sync.dma_start(out=zt_raw[u][:], in_=zt[:, u * N // 2 : (u + 1) * N // 2].rearrange("(p j) n -> p j n", j=PACK))
        nc.sync.dma_start(out=bias[:], in_=b.rearrange("(p t) -> p t", t=PACK))
        load_scale_rows(nc.gpsimd, w_scales[1], wt_scales)

        for page in pages[:2]:
            nc.vector.memset(page[:].bitcast(I32), 0)
        for page in pages[2:]:
            nc.gpsimd.memset(page[:].bitcast(I32), 0)
        nc.gpsimd.tensor_scalar(half_bias[:], bias[:], 0.5, 0.0, ALU.mult, ALU.add)

        w_bank = psum.tile([P, BANK], F32, name="w_bank", tag="diff")
        nc.tensor.transpose(w_bank[:, 0:P], w_rows[:], identity[:])
        nc.vector.tensor_scalar(half_w[:], w_bank[:, 0 : J // P], 0.5, None, ALU.mult)

        def gather(first, count):
            for s in range(2):
                offsets = lists[s][:, first // 16 : (first + count) // 16]
                nc.vector.tensor_copy(picked_scales(s, first, count), table_scales[s][:].indirect(offsets))
                nc.vector.tensor_copy(picked_words(s, first, count), table_words[s][:].bitcast(U32).indirect(offsets))

        def quantise_gate_weight(s, raw_halves, copies):
            grouped = z_grouped[:, s * PACK * N : (s + 1) * PACK * N]
            dealt = grouped.rearrange("p (t m j) -> p m t j", t=PACK, j=PACK)
            for u in range(2):
                copies[u](dealt[:, u * P // 2 : (u + 1) * P // 2], raw_halves[u].rearrange("p j (m t) -> p m t j", t=PACK))
            cols = slice(s * N, (s + 1) * N)
            nc.vector.quantize_mx(out=z_codes[:, cols].bitcast(FP8X4), scales=z_scales[:, cols], in_=grouped)

        branch_weights = (wv_codes[:].bitcast(FP8X4), wt_codes[:].bitcast(FP4X4))

        def branch(s, i):
            h = psum.tile([P, BANK], F32, name="h")
            nc.tensor.matmul_mx(
                out=h[:], lhsT=picked_words(s, i * P, P).bitcast(FP8X4), lhsT_scale=picked_scales(s, i * P, P),
                rhs=branch_weights[s], rhs_scale=w_scales[s][:], start=True, stop=True,
            )
            a = scaled[s][i]
            nc.scalar.activation(a[:].rearrange("p t m -> p m t"), h[:].rearrange("p (m t) -> p m t", t=PACK), ACT.Tanh, scale=1.0 - 2.0 * s)
            nc.scalar.activation(a[:], a[:], ACT.Copy, scale=half_w[:, i : i + 1])

        def branches(i):
            branch(0, i)
            branch(1, i)

        def combine(runs):
            z = psum.tile([P, BANK], F32, name="z")
            text = psum.tile([P, BANK], F32, name="text")
            diff = psum.tile([P, BANK], F32, name="diff", tag="diff")
            gate = ring.tile([P, BANK], F32, name="gate")
            base = ring.tile([P, BANK], F32, name="base")
            gated = ring.tile([P, BANK], F32, name="gated")
            col = 0
            for t, first, count in runs:
                for s in range(2):
                    rows = slice(s * N + t * P, s * N + (t + 1) * P)
                    nc.tensor.matmul_mx(
                        out=z[:, col : col + count], lhsT=z_codes[:, rows].bitcast(FP8X4), lhsT_scale=z_scales[:, rows],
                        rhs=picked_words(s, first, count).bitcast(FP8X4), rhs_scale=picked_scales(s, first, count),
                        start=(s == 0), stop=(s == 1),
                    )
                col += count
            col = 0
            for t, first, count in runs:
                for i in range(first // P, (first + count) // P):
                    nc.tensor.transpose(text[:, col : col + P], scaled[1][i][:, t, :], identity[:])
                    col += P
            col = 0
            for t, first, count in runs:
                for i in range(first // P, (first + count) // P):
                    for s in range(2):
                        nc.tensor.matmul(diff[:, col : col + P], scaled[s][i][:, t, :], identity[:], start=(s == 0), stop=(s == 1), is_transpose=True)
                    col += P
            col = 0
            for t, first, count in runs:
                nc.scalar.activation(gate[:, col : col + count], z[:, col : col + count], ACT.Tanh, bias=half_bias[:, t : t + 1], scale=0.5)
                col += count
            nc.scalar.activation(base[:], text[:], ACT.Copy, scale=-2.0)
            for cols in (slice(0, CHUNK), slice(CHUNK, BANK)):
                nc.vector.scalar_tensor_tensor(gated[:, cols], gate[:, cols], 1.0, diff[:, cols], ALU.add, ALU.mult)
            col = 0
            for t, first, count in runs:
                offsets = list_v[:, first // 16 : (first + count) // 16]
                nc.vector.tensor_tensor(pages[t][:].indirect(offsets), gated[:, col : col + count], base[:, col : col + count], ALU.add)
                col += count

        out_pages = out_0.rearrange("(p t) c -> t p c", t=PACK)

        def store_page(t):
            nc.sync.dma_start(out=out_pages[t], in_=pages[t][:])

        def round_page(t):
            for k, cols in enumerate(blocks):
                slots = pairs[k][:].rearrange("p (u c e) -> p u c e", u=2, e=2)
                copy = nc.vector.tensor_copy if (t >= 2 and k == len(blocks) - 1) else nc.scalar.copy
                copy(slots[:, t // 2, :, t % 2], pages[t][:, cols])

        gather(0, CHUNK)
        quantise_gate_weight(0, [zv_raw[:, :, 0 : N // 2], zv_raw[:, :, N // 2 : N]], [nc.scalar.copy, nc.vector.tensor_copy])
        quantise_gate_weight(1, [zt_raw[0][:], zt_raw[1][:]], [nc.vector.tensor_copy, nc.vector.tensor_copy])
        gather(CHUNK, CHUNK)
        gather(2 * CHUNK, 2 * CHUNK)

        branches(0)
        branches(1)
        combine([(0, 0, CHUNK), (1, 0, CHUNK)])
        combine([(2, 0, CHUNK), (3, 0, CHUNK)])
        branches(2)
        branches(3)
        combine([(0, CHUNK, CHUNK), (1, CHUNK, CHUNK)])
        branches(4)
        combine([(2, CHUNK, CHUNK), (3, CHUNK, CHUNK)])
        branches(5)
        combine([(0, 2 * CHUNK, CHUNK), (1, 2 * CHUNK, CHUNK)])
        branches(6)
        branches(7)
        combine([(0, 3 * CHUNK, CHUNK), (1, 3 * CHUNK, CHUNK)])
        store_page(0)
        store_page(1)
        combine([(2, 2 * CHUNK, 2 * CHUNK)])
        store_page(2)
        combine([(3, 2 * CHUNK, 2 * CHUNK)])
        store_page(3)
        for t in range(PACK):
            round_page(t)

        code_rows = as_words(out_1)

        def interleave(k, copy, word):
            copy(
                y_grouped[k][:].bitcast(word).rearrange("p (c u) -> p c u", u=2),
                pairs[k][:].bitcast(word).rearrange("p (u c) -> p c u", u=2),
            )

        def quantise_block(k):
            nc.vector.quantize_mx(out=y_codes[k][:].bitcast(FP8X4), scales=y_scales[:, blocks[k]], in_=y_grouped[k][:])
            nc.sync.dma_start(out=code_rows[:, blocks[k]], in_=y_codes[k][:].bitcast(I32))

        interleave(3, nc.vector.tensor_copy, I32)
        interleave(0, nc.vector.tensor_copy, I32)
        quantise_block(3)
        interleave(1, nc.vector.tensor_copy, I32)
        quantise_block(0)
        interleave(2, nc.scalar.copy, U32)
        quantise_block(1)
        quantise_block(2)
        for q in range(4):
            nc.scalar.dma_start(out=out_2[0, 4 * q : 4 * q + 4, :].bitcast(I32), in_=y_scales[32 * q : 32 * q + 4, :].bitcast(I32))
